import numpy as np
import ml_dtypes

BF16 = ml_dtypes.bfloat16


def bf(x):
    return np.asarray(x, np.float32).astype(BF16)


def f32(x):
    return np.asarray(x, np.float32)


def f64(x):
    return np.asarray(x).astype(np.float64)


def striped(idx):
    return np.tile(idx.reshape(-1, 16).T, (8, 1))


S, K, M, N, E, Q = 512, 128, 128, 128, 2, 64


def setup_inputs():
    return {"base": bf(np.random.standard_normal((M, S))), "x": bf(np.random.standard_normal((K, N))), "w": bf(np.random.standard_normal((E, K, M)) / np.sqrt(K)), "b": f32(0.5 * np.random.standard_normal((M, 1))), "offs": striped(np.random.permutation(S)[:N])}


def reference(base, x, w, b, offs):
    idx = offs[:16].T.reshape(-1)
    z = f64(base).copy()
    for e in range(E):
        z[:, idx[e * Q : (e + 1) * Q]] += f64(w)[e].T @ f64(x)[:, e * Q : (e + 1) * Q]
    return np.maximum(z + f64(b), 0.0)

@@ -1,0 +1,63 @@
+import concourse.mybir as mybir
+from concourse.masks import make_identity
+
+BF16 = mybir.dt.bfloat16
+F32 = mybir.dt.float32
+U16 = mybir.dt.uint16
+
+P = 128
+TOKENS = 512
+EXPERTS = 2
+PIECE = 64
+ENTRIES = EXPERTS * PIECE
+OFFSETS_PER_COLUMN = 16
+PIECE_COLUMNS = PIECE // OFFSETS_PER_COLUMN
+
+FLOPS = 2 * P * P * ENTRIES
+
+
+def tile_scatter_matmul_kernel(tc, base, x, w, b, offs, out):
+    nc = tc.nc
+    with (
+        tc.tile_pool(name="held", bufs=1) as held,
+        tc.psum_pool(name="psum", bufs=1) as psum,
+    ):
+        base_tile = held.tile([P, TOKENS], BF16)
+        w_tile = held.tile([P, EXPERTS, P], BF16)
+        x_tile = held.tile([P, ENTRIES], BF16)
+        offsets = held.tile([P, ENTRIES // OFFSETS_PER_COLUMN], U16)
+        bias = held.tile([P, 1], F32)
+
+        nc.sync.dma_start(base_tile[:], base)
+        nc.sync.dma_start(w_tile[:], w.rearrange("e k m -> k e m"))
+        nc.sync.dma_start(x_tile[:], x)
+        nc.sync.dma_start(offsets[:], offs)
+        nc.sync.dma_start(bias[:], b)
+
+        identity = held.tile([P, P], BF16)
+        make_identity(nc, identity[:])
+
+        window = psum.tile([P, TOKENS], F32)
+        nc.tensor.matmul(window[:], identity[:], base_tile[:], start=True, stop=False)
+
+        for e in range(EXPERTS):
+            piece = offsets[:, e * PIECE_COLUMNS : (e + 1) * PIECE_COLUMNS]
+            tokens = x_tile[:, e * PIECE : (e + 1) * PIECE]
+            nc.tensor.matmul(
+                window[:].indirect(piece),
+                w_tile[:, e, :],
+                tokens,
+                start=False,
+                stop=e == EXPERTS - 1,
+            )
+
+        result = held.tile([P, TOKENS], F32)
+        nc.vector.tensor_scalar(
+            result[:],
+            window[:],
+            bias[:, 0:1],
+            0.0,
+            op0=mybir.AluOpType.add,
+            op1=mybir.AluOpType.max,
+        )
+        nc.sync.dma_start(out, result[:])

@@ -13,6 +13,8 @@ ENTRIES = EXPERTS * PIECE
 OFFSETS_PER_COLUMN = 16
 PIECE_COLUMNS = PIECE // OFFSETS_PER_COLUMN
 
+WARM_UPS = 4
+
 FLOPS = 2 * P * P * ENTRIES
 
 
@@ -36,6 +38,12 @@ def tile_scatter_matmul_kernel(tc, base, x, w, b, offs, out):
 
         identity = held.tile([P, P], BF16)
         make_identity(nc, identity[:])
+
+        zeros = held.tile([P, TOKENS], BF16)
+        nc.vector.memset(zeros[:], 0.0)
+        unread = psum.tile([P, TOKENS], F32)
+        for warm_up in range(WARM_UPS):
+            nc.tensor.matmul(unread[:], zeros[:, 0:P], zeros[:], start=True, stop=True)
 
         window = psum.tile([P, TOKENS], F32)
         nc.tensor.matmul(window[:], identity[:], base_tile[:], start=True, stop=False)

@@ -13,7 +13,8 @@ ENTRIES = EXPERTS * PIECE
 OFFSETS_PER_COLUMN = 16
 PIECE_COLUMNS = PIECE // OFFSETS_PER_COLUMN
 
-WARM_UPS = 4
+WARM_UP_COLUMNS = 256
+WARM_UPS = 5
 
 FLOPS = 2 * P * P * ENTRIES
 
@@ -39,9 +40,9 @@ def tile_scatter_matmul_kernel(tc, base, x, w, b, offs, out):
         identity = held.tile([P, P], BF16)
         make_identity(nc, identity[:])
 
-        zeros = held.tile([P, TOKENS], BF16)
+        zeros = held.tile([P, WARM_UP_COLUMNS], BF16)
         nc.vector.memset(zeros[:], 0.0)
-        unread = psum.tile([P, TOKENS], F32)
+        unread = psum.tile([P, WARM_UP_COLUMNS], F32)
         for warm_up in range(WARM_UPS):
             nc.tensor.matmul(unread[:], zeros[:, 0:P], zeros[:], start=True, stop=True)
 

import concourse.mybir as mybir
from concourse.masks import make_identity

BF16 = mybir.dt.bfloat16
F32 = mybir.dt.float32
U16 = mybir.dt.uint16

P = 128
TOKENS = 512
EXPERTS = 2
PIECE = 64
ENTRIES = EXPERTS * PIECE
OFFSETS_PER_COLUMN = 16
PIECE_COLUMNS = PIECE // OFFSETS_PER_COLUMN

WARM_UP_COLUMNS = 256
WARM_UPS = 5

FLOPS = 2 * P * P * ENTRIES


def tile_scatter_matmul_kernel(tc, base, x, w, b, offs, out):
    nc = tc.nc
    with (
        tc.tile_pool(name="held", bufs=1) as held,
        tc.psum_pool(name="psum", bufs=1) as psum,
    ):
        base_tile = held.tile([P, TOKENS], BF16)
        w_tile = held.tile([P, EXPERTS, P], BF16)
        x_tile = held.tile([P, ENTRIES], BF16)
        offsets = held.tile([P, ENTRIES // OFFSETS_PER_COLUMN], U16)
        bias = held.tile([P, 1], F32)

        nc.sync.dma_start(base_tile[:], base)
        nc.sync.dma_start(w_tile[:], w.rearrange("e k m -> k e m"))
        nc.sync.dma_start(x_tile[:], x)
        nc.sync.dma_start(offsets[:], offs)
        nc.sync.dma_start(bias[:], b)

        identity = held.tile([P, P], BF16)
        make_identity(nc, identity[:])

        zeros = held.tile([P, WARM_UP_COLUMNS], BF16)
        nc.vector.memset(zeros[:], 0.0)
        unread = psum.tile([P, WARM_UP_COLUMNS], F32)
        for warm_up in range(WARM_UPS):
            nc.tensor.matmul(unread[:], zeros[:, 0:P], zeros[:], start=True, stop=True)

        window = psum.tile([P, TOKENS], F32)
        nc.tensor.matmul(window[:], identity[:], base_tile[:], start=True, stop=False)

        for e in range(EXPERTS):
            piece = offsets[:, e * PIECE_COLUMNS : (e + 1) * PIECE_COLUMNS]
            tokens = x_tile[:, e * PIECE : (e + 1) * PIECE]
            nc.tensor.matmul(
                window[:].indirect(piece),
                w_tile[:, e, :],
                tokens,
                start=False,
                stop=e == EXPERTS - 1,
            )

        result = held.tile([P, TOKENS], F32)
        nc.vector.tensor_scalar(
            result[:],
            window[:],
            bias[:, 0:1],
            0.0,
            op0=mybir.AluOpType.add,
            op1=mybir.AluOpType.max,
        )
        nc.sync.dma_start(out, result[:])
